import numpy as np
import ml_dtypes


def mxq(x, axis, fmt="e4m3"):
    dtype, down = {"e4m3": (ml_dtypes.float8_e4m3fn, 7), "e5m2": (ml_dtypes.float8_e5m2, 14)}[fmt]
    v = np.moveaxis(np.asarray(x, np.float32).astype(ml_dtypes.bfloat16).astype(np.float64), axis, -1)
    blocks = v.reshape(v.shape[:-1] + (-1, 32))
    amax = np.abs(blocks).max(-1, keepdims=True)
    byte = np.maximum(np.where(amax > 0, np.frexp(amax)[1] - 1 + 127, 0) - down, 1)
    scale = np.exp2(byte - 127.0)
    codes = (blocks / scale).astype(np.float32).astype(dtype).astype(np.float64)
    return np.moveaxis((codes * scale).reshape(v.shape), -1, axis)


WIDE = False


def mx_kscale(k):
    if not WIDE:
        return np.ones(k)
    levels = np.array([10, -10, 5, -5, 0])
    if k % 512:
        return np.exp2(np.random.permutation(np.resize(levels, k // 32))).repeat(32)
    a = np.empty((k // 512, 16))
    for p in range(k // 512):
        a[p, :8] = np.random.permutation(np.resize(levels, 8))
        for g in range(8):
            far = levels[np.abs(levels - a[p, g]) >= 10]
            a[p, g + 8] = far[np.random.randint(len(far))]
    return np.exp2(a.ravel()).repeat(32)


def f64(x):
    return np.asarray(x).astype(np.float64)


def striped(idx):
    return np.tile(idx.reshape(-1, 16).T, (8, 1)).astype(np.uint16)


def unstriped(offs):
    return offs[:16].T.reshape(-1).astype(np.int64)


def striped8(idx):
    return np.concatenate([x.reshape(-1, 16).T for x in idx]).astype(np.uint16)


def runs(offs, k):
    lists = np.stack([offs[16 * r : 16 * r + 16].T.reshape(-1) for r in range(8)]).astype(np.int64)
    return lists[np.arange(k) % 512 // 64]


def pack_weight(w):
    k, n = w.shape
    w = f64(np.asarray(w, np.float32).astype(ml_dtypes.bfloat16)).reshape(k // 32, 32, n)
    amax = np.abs(w).max(1)
    byte = np.clip(np.where(amax > 0, np.frexp(amax)[1] - 1 + 127 - 7, 1), 1, 254)
    scaled = (w * np.exp2(127.0 - byte)[:, None, :]).reshape(k, n).astype(np.float32)
    words = np.ascontiguousarray(scaled.reshape(k // 512, 128, 4, n).transpose(0, 1, 3, 2)).astype(ml_dtypes.float8_e4m3fn).view(np.uint8)
    return words, np.ascontiguousarray(byte.astype(np.uint8).reshape(k // 512, 16, n))


def unpack_weight(words, scales):
    g, p, n, _ = words.shape
    vals = np.ascontiguousarray(words).view(ml_dtypes.float8_e4m3fn).astype(np.float64) * np.repeat(np.exp2(scales.astype(np.float64) - 127.0), 8, axis=1)[..., None]
    return vals.transpose(0, 1, 3, 2).reshape(g * 512, n)

def planes(y):
    n, m = y.shape
    v = y.astype(np.float32).astype(ml_dtypes.bfloat16).astype(np.float64).reshape(n // 32, 32, m)
    top = np.abs(v).max(1)
    byte = np.clip(np.where(top > 0, np.frexp(top)[1] - 1 + 127 - 7, 1), 1, 254)
    codes = (v * np.exp2(127.0 - byte)[:, None, :]).reshape(n, m).astype(np.float32).astype(ml_dtypes.float8_e4m3fn).view(np.uint8)
    words = codes.reshape(n // 512, 128, 4, m).transpose(0, 1, 3, 2)
    return np.ascontiguousarray(words), np.ascontiguousarray(byte.astype(np.uint8).reshape(n // 512, 16, m))


K, T, S, V, G, H = 512, 2048, 1024, 512, 2048, 512


def setup_inputs():
    n = np.random.standard_normal
    s = mx_kscale(K)[:, None]
    packed_xT = pack_weight(n((K, T)) * s)
    packed_dT = pack_weight(n((K, G)) / s)
    return {
        "x_words": packed_xT[0],
        "x_scales": packed_xT[1],
        "d_words": packed_dT[0],
        "d_scales": packed_dT[1],
        "gs": (np.random.uniform(0.5, 1.5, (K, 1)) * s).astype(np.float32),
        "offs": striped(np.random.permutation(T)[:S]),
        "k1": striped8(np.random.randint(0, G, (8, H))),
        "n1": striped8(np.stack([np.random.permutation(S) for _ in range(8)])),
        "k2": striped8(np.random.randint(0, G, (8, H))),
        "n2": striped8(np.stack([np.random.permutation(V) for _ in range(8)])),
        "n3": striped8(np.stack([np.random.permutation(V) for _ in range(8)])),
    }


def reference(x_words, x_scales, d_words, d_scales, gs, offs, k1, n1, k2, n2, n3):
    d_k2 = unpack_weight(d_words, d_scales)[np.arange(K)[:, None], runs(k2, K)]
    d_k1 = unpack_weight(d_words, d_scales)[np.arange(K)[:, None], runs(k1, K)]
    xq = unpack_weight(x_words, x_scales)[:, unstriped(offs)]
    h = 0.0625 * (d_k1.T @ xq)
    ln = h[np.arange(H)[:, None], runs(n1, H)]
    mx = ln.reshape(H, V, 2).max(axis=2)
    mn = ln.reshape(H, V, 2).min(axis=2)
    z = f64(gs) * (mx - (0.5 * mn))
    h2 = 0.0625 * ((d_k2.T @ mxq(z, 0, "e4m3")))
    ex = np.exp(h2)
    out_0 = np.log(ex + ex[np.arange(H)[:, None], runs(n2, H)]) - (h2[np.arange(H)[:, None], runs(n3, H)])
    return (out_0,) + planes(out_0)

@@ -1,0 +1,236 @@
+from contextlib import ExitStack
+
+import concourse.mybir as mybir
+
+K, T, S, V, G, H = 512, 2048, 1024, 512, 2048, 512
+FLOPS = 2 * K * H * S + 2 * K * H * V
+
+F32 = mybir.dt.float32
+BF16 = mybir.dt.bfloat16
+I32 = mybir.dt.int32
+U32 = mybir.dt.uint32
+U16 = mybir.dt.uint16
+U8 = mybir.dt.uint8
+FP8X4 = mybir.dt.float8_e4m3fn_x4
+ALU = mybir.AluOpType
+ACT = mybir.ActivationFunctionType
+
+P = 128
+PACK = 4
+BANK = 512
+Z_CHUNKS = ((0, 128), (128, 128), (256, 128), (384, 128))
+OUT_PIECES = ((0, 256), (256, 128), (384, 128))
+HALF = 256
+
+
+def entries(offsets, first, count):
+    return offsets[:, first // 16 : (first + count) // 16]
+
+
+def interleave(engine_copy, dst, src):
+    engine_copy(dst[:].rearrange("p (c i) t -> p c t i", i=4), src[:].rearrange("p t (c i) -> p c t i", i=4))
+
+
+def tile_picked_codepgaplse_none_po_kernel(tc, x_words, x_scales, d_words, d_scales, gs, offs, k1, n1, k2, n2, n3, out_0, out_1, out_2):
+    nc = tc.nc
+    with ExitStack() as ctx:
+        held = ctx.enter_context(tc.tile_pool(name="held", bufs=1))
+        ring = ctx.enter_context(tc.tile_pool(name="ring", bufs=2))
+        psum = ctx.enter_context(tc.psum_pool(name="psum", bufs=8))
+
+        def load_list(name, src):
+            tile = held.tile(list(src.shape), U16, name=name)
+            nc.sync.dma_start(tile[:], src)
+            return tile
+
+        def load_words(name, src):
+            tile = held.tile([P, src.shape[2]], I32, name=name, align_bytes=64)
+            nc.sync.dma_start(tile[:], src[0].rearrange("p n t -> p (n t)").bitcast(I32))
+            return tile
+
+        d_scale_table = held.tile([P, G], U8, align_bytes=64)
+        nc.gpsimd.memset(d_scale_table[:].bitcast(I32), 0)
+        nc.sync.dma_start(d_scale_table[0:P:8, :].bitcast(I32), d_scales[0].bitcast(I32))
+        k1_list = load_list("k1_list", k1)
+        k2_list = load_list("k2_list", k2)
+        offs_list = load_list("offs_list", offs)
+        n1_list = load_list("n1_list", n1)
+        gs_sb = held.tile([P, PACK], F32)
+        nc.sync.dma_start(gs_sb[:], gs.rearrange("(p t) o -> p (t o)", t=PACK))
+        n2_list = load_list("n2_list", n2)
+        n3_list = load_list("n3_list", n3)
+        d_table = load_words("d_table", d_words)
+        x_table = load_words("x_table", x_words)
+
+        x_scale_table = held.tile([P, T], U8, align_bytes=64)
+        nc.gpsimd.memset(x_scale_table[:].bitcast(I32), 0)
+        for q in range(4):
+            nc.gpsimd.dma_start(x_scale_table[32 * q : 32 * q + 4, :].bitcast(I32), x_scales[0, 4 * q : 4 * q + 4, :].bitcast(I32))
+
+        row_factor = held.tile([P, PACK], F32)
+        row_sign = held.tile([P, PACK], F32)
+        nc.scalar.activation(row_factor[:], gs_sb[:], ACT.Copy, scale=0.0625 * 0.25)
+        nc.scalar.activation(row_sign[:], gs_sb[:], ACT.Sign)
+
+        w_scales = held.tile([P, 2 * H], U8, align_bytes=64)
+        nc.vector.memset(w_scales[:].bitcast(I32), 0)
+        picked_scales = held.tile([P, 2 * H], U8, align_bytes=64)
+        dealt_scales = held.tile([P, 2 * H], U8, align_bytes=64)
+        nc.vector.tensor_copy(picked_scales[:, 0:H], d_scale_table[:].indirect(k1_list[:]))
+        nc.vector.tensor_copy(picked_scales[:, H : 2 * H], d_scale_table[:].indirect(k2_list[:]))
+        nc.vector.tensor_copy(
+            dealt_scales[:].rearrange("p (l t m) -> p l t m", l=2, t=PACK),
+            picked_scales[:].rearrange("p (l m t) -> p l t m", l=2, t=PACK),
+        )
+        for r in range(4):
+            nc.sync.dma_start(w_scales[r:P:32, :].bitcast(I32), dealt_scales[8 * r : P : 32, :].bitcast(I32))
+
+        def pick_weights(name, k_list, slot):
+            picked = held.tile([P, H], U32, name=name + "_picked", tag=slot, align_bytes=64)
+            dealt = held.tile([P, H], U32, name=name + "_dealt", align_bytes=64)
+            nc.vector.tensor_copy(picked[:], d_table[:].bitcast(U32).indirect(k_list[:]))
+            nc.vector.tensor_copy(dealt[:].rearrange("p (t m) -> p t m", t=PACK), picked[:].rearrange("p (m t) -> p t m", t=PACK))
+            return dealt
+
+        w1_words = pick_weights("w1", k1_list, "w1_picked")
+
+        h_rows = [held.tile([P, S], F32, name=f"h_rows{t}") for t in range(PACK)]
+        h_banks = {}
+        for half in range(S // BANK):
+            picks = entries(offs_list, half * BANK, BANK)
+            xq_scales = held.tile([P, BANK], U8, name=f"xq_scales{half}", align_bytes=64)
+            xq_words = held.tile([P, BANK], U32, name=f"xq_words{half}", tag=f"xq_words{half}", align_bytes=64)
+            nc.vector.tensor_copy(xq_scales[:], x_scale_table[:].indirect(picks))
+            nc.vector.tensor_copy(xq_words[:], x_table[:].bitcast(U32).indirect(picks))
+            for t in range(PACK):
+                acc = psum.tile([P, BANK], F32, tag="bank")
+                nc.tensor.matmul_mx(
+                    acc[:],
+                    lhsT=w1_words[:, t * P : (t + 1) * P].bitcast(FP8X4),
+                    lhsT_scale=w_scales[:, t * P : (t + 1) * P],
+                    rhs=xq_words[:].bitcast(FP8X4),
+                    rhs_scale=xq_scales[:],
+                    start=True,
+                    stop=True,
+                )
+                h_banks[t, half] = acc
+        for t, half in ((0, 0), (1, 0), (0, 1), (1, 1), (2, 0), (2, 1), (3, 0), (3, 1)):
+            nc.scalar.activation(h_rows[t][:, half * BANK : (half + 1) * BANK], h_banks[t, half][:], ACT.Copy, scale=row_factor[:, t : t + 1])
+
+        w2_words = pick_weights("w2", k2_list, "xq_words0")
+
+        ex_rows = [held.tile([P, V], F32, name=f"ex_rows{t}") for t in range(PACK)]
+        neg_h2_rows = [held.tile([P, V], F32, name=f"neg_h2_rows{t}") for t in range(PACK)]
+        ex_plain = held.tile([P, PACK, V], F32)
+
+        units = []
+        for c, (v0, n) in enumerate(Z_CHUNKS):
+            per = HALF // n
+            for t0 in range(0, PACK, per):
+                units.append((c, list(range(t0, t0 + per))))
+        z_planes = [held.tile([P, PACK, n], BF16, name=f"z_planes{c}") for c, (v0, n) in enumerate(Z_CHUNKS)]
+        lined, sums, gaps, h2_banks = {}, {}, {}, {}
+
+        def line_up(u):
+            c, ts = units[u]
+            v0, n = Z_CHUNKS[c]
+            ln = ring.tile([P, 2 * HALF], F32, tag="ln")
+            for i, t in enumerate(ts):
+                nc.vector.tensor_copy(ln[:, 2 * n * i : 2 * n * (i + 1)], h_rows[t][:].indirect(entries(n1_list, 2 * v0, 2 * n)))
+            pair_sum = ring.tile([P, HALF], F32, tag="pair_sum")
+            nc.gpsimd.tensor_tensor(pair_sum[:], ln[:, 0 : 2 * HALF : 2], ln[:, 1 : 2 * HALF : 2], ALU.add)
+            lined[u] = ln
+            sums[u] = pair_sum
+
+        def differ(u):
+            diff = ring.tile([P, HALF], F32, tag="diff")
+            nc.vector.scalar_tensor_tensor(diff[:], lined[u][:, 1 : 2 * HALF : 2], -2.0, sums[u][:], ALU.mult, ALU.add)
+            gap = ring.tile([P, HALF], F32, tag="gap")
+            nc.scalar.activation(gap[:], diff[:], ACT.Abs, scale=3.0)
+            gaps[u] = gap
+
+        def combine(u):
+            c, ts = units[u]
+            v0, n = Z_CHUNKS[c]
+            for i, t in enumerate(ts):
+                cols = slice(n * i, n * (i + 1))
+                nc.vector.scalar_tensor_tensor(z_planes[c][:, t, :], gaps[u][:, cols], row_sign[:, t : t + 1], sums[u][:, cols], ALU.mult, ALU.add)
+            if ts[-1] == PACK - 1:
+                second_product(c)
+
+        def second_product(c):
+            v0, n = Z_CHUNKS[c]
+            z_grouped = held.tile([P, n, PACK], BF16, name=f"z_grouped{c}", align_bytes=64)
+            interleave(nc.vector.tensor_copy if c == len(Z_CHUNKS) - 1 else nc.scalar.copy, z_grouped, z_planes[c])
+            z_words = held.tile([P, n], U32, name=f"z_words{c}", align_bytes=64)
+            z_scales = held.tile([P, n], U8, name=f"z_scales{c}", align_bytes=64)
+            nc.vector.quantize_mx(z_words[:].bitcast(FP8X4), z_scales[:], z_grouped[:].rearrange("p v t -> p (v t)"))
+            acc = psum.tile([P, PACK, n], F32, tag="bank")
+            for t in range(PACK):
+                nc.tensor.matmul_mx(
+                    acc[:, t, :],
+                    lhsT=w2_words[:, t * P : (t + 1) * P].bitcast(FP8X4),
+                    lhsT_scale=w_scales[:, H + t * P : H + (t + 1) * P],
+                    rhs=z_words[:].bitcast(FP8X4),
+                    rhs_scale=z_scales[:],
+                    start=True,
+                    stop=True,
+                )
+            h2_banks[c] = acc
+
+        def exponentiate(c):
+            v0, n = Z_CHUNKS[c]
+            cols = slice(v0, v0 + n)
+            for t in range(PACK):
+                nc.scalar.activation(ex_rows[t][:, cols], h2_banks[c][:, t, :], ACT.Exp, scale=0.0625)
+            if c == len(Z_CHUNKS) - 1:
+                nc.scalar.activation(ex_plain[:, :, cols], h2_banks[c][:], ACT.Exp, scale=0.0625)
+            elif c > 0:
+                first = 0 if c == 1 else v0
+                for t in range(PACK):
+                    nc.sync.dma_start(ex_plain[:, t, first : v0 + n], ex_rows[t][:, first : v0 + n])
+
+        def negate(c):
+            v0, n = Z_CHUNKS[c]
+            for t in range(PACK):
+                nc.scalar.activation(neg_h2_rows[t][:, v0 : v0 + n], h2_banks[c][:, t, :], ACT.Copy, scale=-0.0625)
+
+        for step in range(len(units) + 4):
+            if step < len(units):
+                line_up(step)
+            if 0 <= step - 1 < len(units):
+                differ(step - 1)
+            if 0 <= step - 2 < len(units):
+                combine(step - 2)
+            if step >= 4 and step % 2 == 0:
+                exponentiate((step - 4) // 2)
+            if step >= 5 and step % 2 == 1:
+                negate((step - 5) // 2)
+
+        log_sum = held.tile([P, PACK, V], F32)
+        for half in range(V // HALF):
+            cols = slice(half * HALF, (half + 1) * HALF)
+            for t0 in range(0, PACK, 2):
+                ex_sum = held.tile([P, 2, HALF], F32, name=f"ex_sum{half}_{t0}")
+                for i in range(2):
+                    t = t0 + i
+                    nc.vector.tensor_tensor(ex_sum[:, i, :], ex_rows[t][:].indirect(entries(n2_list, half * HALF, HALF)), ex_plain[:, t, cols], ALU.add)
+                nc.scalar.activation(log_sum[:, t0 : t0 + 2, cols], ex_sum[:], ACT.Ln)
+
+        out_rows = out_0.rearrange("(p t) v -> p t v", t=PACK)
+        out_words = out_1[0].rearrange("p n t -> p (n t)").bitcast(I32)
+        y_scales = held.tile([P, V], U8, align_bytes=64)
+        for j, (v0, n) in enumerate(OUT_PIECES):
+            cols = slice(v0, v0 + n)
+            y = held.tile([P, PACK, n], F32, name=f"y{j}")
+            for t in range(PACK):
+                nc.vector.tensor_tensor(y[:, t, :], neg_h2_rows[t][:].indirect(entries(n3_list, v0, n)), log_sum[:, t, cols], ALU.add)
+            nc.sync.dma_start(out_rows[:, :, cols], y[:])
+            y_grouped = held.tile([P, n, PACK], BF16, name=f"y_grouped{j}", align_bytes=64)
+            interleave(nc.vector.tensor_copy if j == len(OUT_PIECES) - 1 else nc.scalar.copy, y_grouped, y)
+            y_words = held.tile([P, n], U32, name=f"y_words{j}", align_bytes=64)
+            nc.vector.quantize_mx(y_words[:].bitcast(FP8X4), y_scales[:, cols], y_grouped[:].rearrange("p v t -> p (v t)"))
+            nc.sync.dma_start(out_words[:, cols], y_words[:].bitcast(I32))
+        for q in range(4):
+            queue = nc.scalar if q % 2 else nc.sync
+            queue.dma_start(out_2[0, 4 * q : 4 * q + 4, :].bitcast(I32), y_scales[32 * q : 32 * q + 4, :].bitcast(I32))

@@ -18,7 +18,7 @@ ACT = mybir.ActivationFunctionType
 P = 128
 PACK = 4
 BANK = 512
-Z_CHUNKS = ((0, 128), (128, 128), (256, 128), (384, 128))
+Z_CHUNKS = ((0, 256), (256, 128), (384, 128))
 OUT_PIECES = ((0, 256), (256, 128), (384, 128))
 HALF = 256
 
@@ -51,6 +51,9 @@ def tile_picked_codepgaplse_none_po_kernel(tc, x_words, x_scales, d_words, d_sca
         d_scale_table = held.tile([P, G], U8, align_bytes=64)
         nc.gpsimd.memset(d_scale_table[:].bitcast(I32), 0)
         nc.sync.dma_start(d_scale_table[0:P:8, :].bitcast(I32), d_scales[0].bitcast(I32))
+        x_scale_table = held.tile([P, T], U8, align_bytes=64)
+        nc.vector.memset(x_scale_table[:].bitcast(I32), 0)
+        nc.sync.dma_start(x_scale_table[0:P:8, :].bitcast(I32), x_scales[0].bitcast(I32))
         k1_list = load_list("k1_list", k1)
         k2_list = load_list("k2_list", k2)
         offs_list = load_list("offs_list", offs)
@@ -62,18 +65,13 @@ def tile_picked_codepgaplse_none_po_kernel(tc, x_words, x_scales, d_words, d_sca
         d_table = load_words("d_table", d_words)
         x_table = load_words("x_table", x_words)
 
-        x_scale_table = held.tile([P, T], U8, align_bytes=64)
-        nc.gpsimd.memset(x_scale_table[:].bitcast(I32), 0)
-        for q in range(4):
-            nc.gpsimd.dma_start(x_scale_table[32 * q : 32 * q + 4, :].bitcast(I32), x_scales[0, 4 * q : 4 * q + 4, :].bitcast(I32))
-
         row_factor = held.tile([P, PACK], F32)
         row_sign = held.tile([P, PACK], F32)
         nc.scalar.activation(row_factor[:], gs_sb[:], ACT.Copy, scale=0.0625 * 0.25)
         nc.scalar.activation(row_sign[:], gs_sb[:], ACT.Sign)
 
         w_scales = held.tile([P, 2 * H], U8, align_bytes=64)
-        nc.vector.memset(w_scales[:].bitcast(I32), 0)
+        nc.gpsimd.memset(w_scales[:].bitcast(I32), 0)
         picked_scales = held.tile([P, 2 * H], U8, align_bytes=64)
         dealt_scales = held.tile([P, 2 * H], U8, align_bytes=64)
         nc.vector.tensor_copy(picked_scales[:, 0:H], d_scale_table[:].indirect(k1_list[:]))
@@ -84,6 +82,13 @@ def tile_picked_codepgaplse_none_po_kernel(tc, x_words, x_scales, d_words, d_sca
         )
         for r in range(4):
             nc.sync.dma_start(w_scales[r:P:32, :].bitcast(I32), dealt_scales[8 * r : P : 32, :].bitcast(I32))
+
+        xq_scales = held.tile([P, S], U8, align_bytes=64)
+        nc.gpsimd.memset(xq_scales[:].bitcast(I32), 0)
+        picked_x_scales = held.tile([P, S], U8, align_bytes=64)
+        nc.vector.tensor_copy(picked_x_scales[:], x_scale_table[:].indirect(offs_list[:]))
+        for r in range(4):
+            nc.sync.dma_start(xq_scales[r:P:32, :].bitcast(I32), picked_x_scales[8 * r : P : 32, :].bitcast(I32))
 
         def pick_weights(name, k_list, slot):
             picked = held.tile([P, H], U32, name=name + "_picked", tag=slot, align_bytes=64)
@@ -98,9 +103,7 @@ def tile_picked_codepgaplse_none_po_kernel(tc, x_words, x_scales, d_words, d_sca
         h_banks = {}
         for half in range(S // BANK):
             picks = entries(offs_list, half * BANK, BANK)
-            xq_scales = held.tile([P, BANK], U8, name=f"xq_scales{half}", align_bytes=64)
             xq_words = held.tile([P, BANK], U32, name=f"xq_words{half}", tag=f"xq_words{half}", align_bytes=64)
-            nc.vector.tensor_copy(xq_scales[:], x_scale_table[:].indirect(picks))
             nc.vector.tensor_copy(xq_words[:], x_table[:].bitcast(U32).indirect(picks))
             for t in range(PACK):
                 acc = psum.tile([P, BANK], F32, tag="bank")
@@ -109,7 +112,7 @@ def tile_picked_codepgaplse_none_po_kernel(tc, x_words, x_scales, d_words, d_sca
                     lhsT=w1_words[:, t * P : (t + 1) * P].bitcast(FP8X4),
                     lhsT_scale=w_scales[:, t * P : (t + 1) * P],
                     rhs=xq_words[:].bitcast(FP8X4),
-                    rhs_scale=xq_scales[:],
+                    rhs_scale=xq_scales[:, half * BANK : (half + 1) * BANK],
                     start=True,
                     stop=True,
                 )
@@ -129,7 +132,7 @@ def tile_picked_codepgaplse_none_po_kernel(tc, x_words, x_scales, d_words, d_sca
             for t0 in range(0, PACK, per):
                 units.append((c, list(range(t0, t0 + per))))
         z_planes = [held.tile([P, PACK, n], BF16, name=f"z_planes{c}") for c, (v0, n) in enumerate(Z_CHUNKS)]
-        lined, sums, gaps, h2_banks = {}, {}, {}, {}
+        lined, sums, gaps, h2_banks, h2_sums = {}, {}, {}, {}, {}
 
         def line_up(u):
             c, ts = units[u]
@@ -137,14 +140,15 @@ def tile_picked_codepgaplse_none_po_kernel(tc, x_words, x_scales, d_words, d_sca
             ln = ring.tile([P, 2 * HALF], F32, tag="ln")
             for i, t in enumerate(ts):
                 nc.vector.tensor_copy(ln[:, 2 * n * i : 2 * n * (i + 1)], h_rows[t][:].indirect(entries(n1_list, 2 * v0, 2 * n)))
-            pair_sum = ring.tile([P, HALF], F32, tag="pair_sum")
-            nc.gpsimd.tensor_tensor(pair_sum[:], ln[:, 0 : 2 * HALF : 2], ln[:, 1 : 2 * HALF : 2], ALU.add)
             lined[u] = ln
-            sums[u] = pair_sum
 
         def differ(u):
+            first, second = lined[u][:, 0 : 2 * HALF : 2], lined[u][:, 1 : 2 * HALF : 2]
             diff = ring.tile([P, HALF], F32, tag="diff")
-            nc.vector.scalar_tensor_tensor(diff[:], lined[u][:, 1 : 2 * HALF : 2], -2.0, sums[u][:], ALU.mult, ALU.add)
+            nc.vector.tensor_tensor(diff[:], first, second, ALU.subtract)
+            pair_sum = ring.tile([P, HALF], F32, tag="pair_sum")
+            nc.vector.tensor_tensor(pair_sum[:], first, second, ALU.add)
+            sums[u] = pair_sum
             gap = ring.tile([P, HALF], F32, tag="gap")
             nc.scalar.activation(gap[:], diff[:], ACT.Abs, scale=3.0)
             gaps[u] = gap
@@ -165,10 +169,12 @@ def tile_picked_codepgaplse_none_po_kernel(tc, x_words, x_scales, d_words, d_sca
             z_words = held.tile([P, n], U32, name=f"z_words{c}", align_bytes=64)
             z_scales = held.tile([P, n], U8, name=f"z_scales{c}", align_bytes=64)
             nc.vector.quantize_mx(z_words[:].bitcast(FP8X4), z_scales[:], z_grouped[:].rearrange("p v t -> p (v t)"))
-            acc = psum.tile([P, PACK, n], F32, tag="bank")
+            per_bank = BANK // n
             for t in range(PACK):
+                if t % per_bank == 0:
+                    acc = psum.tile([P, per_bank, n], F32, tag="bank")
                 nc.tensor.matmul_mx(
-                    acc[:, t, :],
+                    acc[:, t % per_bank, :],
                     lhsT=w2_words[:, t * P : (t + 1) * P].bitcast(FP8X4),
                     lhsT_scale=w_scales[:, H + t * P : H + (t + 1) * P],
                     rhs=z_words[:].bitcast(FP8X4),
@@ -176,25 +182,26 @@ def tile_picked_codepgaplse_none_po_kernel(tc, x_words, x_scales, d_words, d_sca
                     start=True,
                     stop=True,
                 )
+                h2_sums[c, t] = acc[:, t % per_bank, :]
             h2_banks[c] = acc
 
         def exponentiate(c):
             v0, n = Z_CHUNKS[c]
             cols = slice(v0, v0 + n)
             for t in range(PACK):
-                nc.scalar.activation(ex_rows[t][:, cols], h2_banks[c][:, t, :], ACT.Exp, scale=0.0625)
+                nc.scalar.activation(ex_rows[t][:, cols], h2_sums[c, t], ACT.Exp, scale=0.0625)
             if c == len(Z_CHUNKS) - 1:
                 nc.scalar.activation(ex_plain[:, :, cols], h2_banks[c][:], ACT.Exp, scale=0.0625)
-            elif c > 0:
-                first = 0 if c == 1 else v0
+            else:
                 for t in range(PACK):
-                    nc.sync.dma_start(ex_plain[:, t, first : v0 + n], ex_rows[t][:, first : v0 + n])
+                    nc.sync.dma_start(ex_plain[:, t, cols], ex_rows[t][:, cols])
 
         def negate(c):
             v0, n = Z_CHUNKS[c]
             for t in range(PACK):
-                nc.scalar.activation(neg_h2_rows[t][:, v0 : v0 + n], h2_banks[c][:, t, :], ACT.Copy, scale=-0.0625)
+                nc.scalar.activation(neg_h2_rows[t][:, v0 : v0 + n], h2_sums[c, t], ACT.Copy, scale=-0.0625)
 
+        last_unit = {c: u for u, (c, ts) in enumerate(units)}
         for step in range(len(units) + 4):
             if step < len(units):
                 line_up(step)
@@ -202,10 +209,11 @@ def tile_picked_codepgaplse_none_po_kernel(tc, x_words, x_scales, d_words, d_sca
                 differ(step - 1)
             if 0 <= step - 2 < len(units):
                 combine(step - 2)
-            if step >= 4 and step % 2 == 0:
-                exponentiate((step - 4) // 2)
-            if step >= 5 and step % 2 == 1:
-                negate((step - 5) // 2)
+            for c, u in last_unit.items():
+                if step == u + 3:
+                    exponentiate(c)
+                if step == u + 4:
+                    negate(c)
 
         log_sum = held.tile([P, PACK, V], F32)
         for half in range(V // HALF):

@@ -1,6 +1,7 @@
 from contextlib import ExitStack
 
 import concourse.mybir as mybir
+from concourse.masks import make_identity
 
 K, T, S, V, G, H = 512, 2048, 1024, 512, 2048, 512
 FLOPS = 2 * K * H * S + 2 * K * H * V
@@ -21,6 +22,7 @@ BANK = 512
 Z_CHUNKS = ((0, 256), (256, 128), (384, 128))
 OUT_PIECES = ((0, 256), (256, 128), (384, 128))
 HALF = 256
+PE_UNITS = 7
 
 
 def entries(offsets, first, count):
@@ -28,7 +30,7 @@ def entries(offsets, first, count):
 
 
 def interleave(engine_copy, dst, src):
-    engine_copy(dst[:].rearrange("p (c i) t -> p c t i", i=4), src[:].rearrange("p t (c i) -> p c t i", i=4))
+    engine_copy(dst.rearrange("p (c i) t -> p c t i", i=4), src.rearrange("p t (c i) -> p c t i", i=4))
 
 
 def tile_picked_codepgaplse_none_po_kernel(tc, x_words, x_scales, d_words, d_scales, gs, offs, k1, n1, k2, n2, n3, out_0, out_1, out_2):
@@ -44,11 +46,11 @@ def tile_picked_codepgaplse_none_po_kernel(tc, x_words, x_scales, d_words, d_sca
             return tile
 
         def load_words(name, src):
-            tile = held.tile([P, src.shape[2]], I32, name=name, align_bytes=64)
+            tile = held.tile([P, src.shape[2]], I32, name=name, tag=name, align_bytes=64)
             nc.sync.dma_start(tile[:], src[0].rearrange("p n t -> p (n t)").bitcast(I32))
             return tile
 
-        d_scale_table = held.tile([P, G], U8, align_bytes=64)
+        d_scale_table = held.tile([P, G], U8, tag="d_scale_table", align_bytes=64)
         nc.gpsimd.memset(d_scale_table[:].bitcast(I32), 0)
         nc.sync.dma_start(d_scale_table[0:P:8, :].bitcast(I32), d_scales[0].bitcast(I32))
         x_scale_table = held.tile([P, T], U8, align_bytes=64)
@@ -58,69 +60,66 @@ def tile_picked_codepgaplse_none_po_kernel(tc, x_words, x_scales, d_words, d_sca
         k2_list = load_list("k2_list", k2)
         offs_list = load_list("offs_list", offs)
         n1_list = load_list("n1_list", n1)
-        gs_sb = held.tile([P, PACK], F32)
-        nc.sync.dma_start(gs_sb[:], gs.rearrange("(p t) o -> p (t o)", t=PACK))
         n2_list = load_list("n2_list", n2)
         n3_list = load_list("n3_list", n3)
         d_table = load_words("d_table", d_words)
         x_table = load_words("x_table", x_words)
 
+        placed_scales = held.tile([P, 2 * H + S], U8, align_bytes=64)
+        nc.gpsimd.memset(placed_scales[:].bitcast(I32), 0)
+        picked_scales = held.tile([P, 2 * H + S], U8, align_bytes=64)
+        nc.vector.tensor_copy(picked_scales[:, 0:H], d_scale_table[:].indirect(k1_list[:]))
+        nc.vector.tensor_copy(picked_scales[:, H : 2 * H], d_scale_table[:].indirect(k2_list[:]))
+        staged_scales = held.tile([P, 2 * H + S], U8, align_bytes=64)
+        nc.vector.tensor_copy(
+            staged_scales[:, 0 : 2 * H].rearrange("p (l t m) -> p l m t", l=2, t=PACK),
+            picked_scales[:, 0 : 2 * H].rearrange("p (l m t) -> p l m t", l=2, t=PACK),
+        )
+        nc.vector.tensor_copy(picked_scales[:, 2 * H :], x_scale_table[:].indirect(offs_list[:]))
+        nc.vector.tensor_copy(staged_scales[:, 2 * H :].bitcast(I32), picked_scales[:, 2 * H :].bitcast(I32))
+        for r in range(4):
+            nc.sync.dma_start(placed_scales[r:P:32, :].bitcast(I32), staged_scales[8 * r : P : 32, :].bitcast(I32))
+
+        gs_sb = held.tile([P, PACK], F32, tag="d_scale_table", align_bytes=64)
+        nc.sync.dma_start(gs_sb[:], gs.rearrange("(p t) o -> p (t o)", t=PACK))
         row_factor = held.tile([P, PACK], F32)
         row_sign = held.tile([P, PACK], F32)
         nc.scalar.activation(row_factor[:], gs_sb[:], ACT.Copy, scale=0.0625 * 0.25)
         nc.scalar.activation(row_sign[:], gs_sb[:], ACT.Sign)
 
-        w_scales = held.tile([P, 2 * H], U8, align_bytes=64)
-        nc.gpsimd.memset(w_scales[:].bitcast(I32), 0)
-        picked_scales = held.tile([P, 2 * H], U8, align_bytes=64)
-        dealt_scales = held.tile([P, 2 * H], U8, align_bytes=64)
-        nc.vector.tensor_copy(picked_scales[:, 0:H], d_scale_table[:].indirect(k1_list[:]))
-        nc.vector.tensor_copy(picked_scales[:, H : 2 * H], d_scale_table[:].indirect(k2_list[:]))
-        nc.vector.tensor_copy(
-            dealt_scales[:].rearrange("p (l t m) -> p l t m", l=2, t=PACK),
-            picked_scales[:].rearrange("p (l m t) -> p l t m", l=2, t=PACK),
-        )
-        for r in range(4):
-            nc.sync.dma_start(w_scales[r:P:32, :].bitcast(I32), dealt_scales[8 * r : P : 32, :].bitcast(I32))
-
-        xq_scales = held.tile([P, S], U8, align_bytes=64)
-        nc.gpsimd.memset(xq_scales[:].bitcast(I32), 0)
-        picked_x_scales = held.tile([P, S], U8, align_bytes=64)
-        nc.vector.tensor_copy(picked_x_scales[:], x_scale_table[:].indirect(offs_list[:]))
-        for r in range(4):
-            nc.sync.dma_start(xq_scales[r:P:32, :].bitcast(I32), picked_x_scales[8 * r : P : 32, :].bitcast(I32))
+        identity = held.tile([P, P], F32)
+        make_identity(nc, identity[:])
 
         def pick_weights(name, k_list, slot):
             picked = held.tile([P, H], U32, name=name + "_picked", tag=slot, align_bytes=64)
             dealt = held.tile([P, H], U32, name=name + "_dealt", align_bytes=64)
             nc.vector.tensor_copy(picked[:], d_table[:].bitcast(U32).indirect(k_list[:]))
-            nc.vector.tensor_copy(dealt[:].rearrange("p (t m) -> p t m", t=PACK), picked[:].rearrange("p (m t) -> p t m", t=PACK))
+            nc.vector.tensor_copy(dealt[:].rearrange("p (t m) -> p m t", t=PACK), picked[:].rearrange("p (m t) -> p m t", t=PACK))
             return dealt
 
         w1_words = pick_weights("w1", k1_list, "w1_picked")
+        xq_words = []
+        for half in range(S // BANK):
+            words = held.tile([P, BANK], U32, name=f"xq_words{half}", align_bytes=64)
+            nc.vector.tensor_copy(words[:], x_table[:].bitcast(U32).indirect(entries(offs_list, half * BANK, BANK)))
+            xq_words.append(words)
+        w2_words = pick_weights("w2", k2_list, "x_table")
 
         h_rows = [held.tile([P, S], F32, name=f"h_rows{t}") for t in range(PACK)]
-        h_banks = {}
-        for half in range(S // BANK):
-            picks = entries(offs_list, half * BANK, BANK)
-            xq_words = held.tile([P, BANK], U32, name=f"xq_words{half}", tag=f"xq_words{half}", align_bytes=64)
-            nc.vector.tensor_copy(xq_words[:], x_table[:].bitcast(U32).indirect(picks))
-            for t in range(PACK):
+
+        def first_product(*parts):
+            for t, half in parts:
                 acc = psum.tile([P, BANK], F32, tag="bank")
                 nc.tensor.matmul_mx(
                     acc[:],
                     lhsT=w1_words[:, t * P : (t + 1) * P].bitcast(FP8X4),
-                    lhsT_scale=w_scales[:, t * P : (t + 1) * P],
-                    rhs=xq_words[:].bitcast(FP8X4),
-                    rhs_scale=xq_scales[:, half * BANK : (half + 1) * BANK],
+                    lhsT_scale=placed_scales[:, t * P : (t + 1) * P],
+                    rhs=xq_words[half][:].bitcast(FP8X4),
+                    rhs_scale=placed_scales[:, 2 * H + half * BANK : 2 * H + (half + 1) * BANK],
                     start=True,
                     stop=True,
                 )
-                h_banks[t, half] = acc
-        for t, half in ((0, 0), (1, 0), (0, 1), (1, 1), (2, 0), (2, 1), (3, 0), (3, 1)):
-            nc.scalar.activation(h_rows[t][:, half * BANK : (half + 1) * BANK], h_banks[t, half][:], ACT.Copy, scale=row_factor[:, t : t + 1])
-
-        w2_words = pick_weights("w2", k2_list, "xq_words0")
+                nc.scalar.activation(h_rows[t][:, half * BANK : (half + 1) * BANK], acc[:], ACT.Copy, scale=row_factor[:, t : t + 1])
 
         ex_rows = [held.tile([P, V], F32, name=f"ex_rows{t}") for t in range(PACK)]
         neg_h2_rows = [held.tile([P, V], F32, name=f"neg_h2_rows{t}") for t in range(PACK)]
@@ -137,19 +136,33 @@ def tile_picked_codepgaplse_none_po_kernel(tc, x_words, x_scales, d_words, d_sca
         def line_up(u):
             c, ts = units[u]
             v0, n = Z_CHUNKS[c]
-            ln = ring.tile([P, 2 * HALF], F32, tag="ln")
+            ln = held.tile([P, 2 * HALF], F32, tag=f"slot{u % 3}" if u < 7 else "z_grouped0", align_bytes=64)
             for i, t in enumerate(ts):
                 nc.vector.tensor_copy(ln[:, 2 * n * i : 2 * n * (i + 1)], h_rows[t][:].indirect(entries(n1_list, 2 * v0, 2 * n)))
             lined[u] = ln
 
+        def add_up(u):
+            ln = lined[u]
+            if u < PE_UNITS:
+                turned = psum.tile([P, 2, P], F32, tag="bank")
+                for b in range(2):
+                    for e in range(2):
+                        nc.tensor.matmul(turned[:, b, :], ln[:, 2 * P * b + e : 2 * P * (b + 1) : 2], identity[:], start=e == 0, stop=e == 1, is_transpose=True)
+                turned_sb = ring.tile([P, 2, P], F32, tag="turned_sb")
+                nc.scalar.copy(turned_sb[:], turned[:])
+                pair_sum = psum.tile([P, HALF], F32, tag="bank")
+                for b in range(2):
+                    nc.tensor.transpose(pair_sum[:, P * b : P * (b + 1)], turned_sb[:, b, :], identity[:])
+            else:
+                pair_sum = ring.tile([P, HALF], F32, tag="pair_sum")
+                nc.vector.tensor_tensor(pair_sum[:], ln[:, 0 : 2 * HALF : 2], ln[:, 1 : 2 * HALF : 2], ALU.add)
+            sums[u] = pair_sum
+
         def differ(u):
             first, second = lined[u][:, 0 : 2 * HALF : 2], lined[u][:, 1 : 2 * HALF : 2]
-            diff = ring.tile([P, HALF], F32, tag="diff")
+            diff = held.tile([P, HALF], F32, tag="diff" if u < 7 else "last_diff")
             nc.vector.tensor_tensor(diff[:], first, second, ALU.subtract)
-            pair_sum = ring.tile([P, HALF], F32, tag="pair_sum")
-            nc.vector.tensor_tensor(pair_sum[:], first, second, ALU.add)
-            sums[u] = pair_sum
-            gap = ring.tile([P, HALF], F32, tag="gap")
+            gap = held.tile([P, HALF], F32, tag=f"slot{u % 3}" if u + 3 < 7 else f"gap{u}", align_bytes=64)
             nc.scalar.activation(gap[:], diff[:], ACT.Abs, scale=3.0)
             gaps[u] = gap
 
@@ -159,13 +172,12 @@ def tile_picked_codepgaplse_none_po_kernel(tc, x_words, x_scales, d_words, d_sca
             for i, t in enumerate(ts):
                 cols = slice(n * i, n * (i + 1))
                 nc.vector.scalar_tensor_tensor(z_planes[c][:, t, :], gaps[u][:, cols], row_sign[:, t : t + 1], sums[u][:, cols], ALU.mult, ALU.add)
-            if ts[-1] == PACK - 1:
-                second_product(c)
 
         def second_product(c):
             v0, n = Z_CHUNKS[c]
-            z_grouped = held.tile([P, n, PACK], BF16, name=f"z_grouped{c}", align_bytes=64)
-            interleave(nc.vector.tensor_copy if c == len(Z_CHUNKS) - 1 else nc.scalar.copy, z_grouped, z_planes[c])
+            z_grouped = held.tile([P, n, PACK], BF16, name=f"z_grouped{c}", tag=f"z_grouped{c}", align_bytes=64)
+            for w0 in range(0, n, P):
+                interleave(nc.vector.tensor_copy if c == len(Z_CHUNKS) - 1 else nc.scalar.copy, z_grouped[:, w0 : w0 + P, :], z_planes[c][:, :, w0 : w0 + P])
             z_words = held.tile([P, n], U32, name=f"z_words{c}", align_bytes=64)
             z_scales = held.tile([P, n], U8, name=f"z_scales{c}", align_bytes=64)
             nc.vector.quantize_mx(z_words[:].bitcast(FP8X4), z_scales[:], z_grouped[:].rearrange("p v t -> p (v t)"))
@@ -176,7 +188,7 @@ def tile_picked_codepgaplse_none_po_kernel(tc, x_words, x_scales, d_words, d_sca
                 nc.tensor.matmul_mx(
                     acc[:, t % per_bank, :],
                     lhsT=w2_words[:, t * P : (t + 1) * P].bitcast(FP8X4),
-                    lhsT_scale=w_scales[:, H + t * P : H + (t + 1) * P],
+                    lhsT_scale=placed_scales[:, H + t * P : H + (t + 1) * P],
                     rhs=z_words[:].bitcast(FP8X4),
                     rhs_scale=z_scales[:],
                     start=True,
@@ -185,35 +197,57 @@ def tile_picked_codepgaplse_none_po_kernel(tc, x_words, x_scales, d_words, d_sca
                 h2_sums[c, t] = acc[:, t % per_bank, :]
             h2_banks[c] = acc
 
-        def exponentiate(c):
+        def exponentiate(c, ts):
             v0, n = Z_CHUNKS[c]
             cols = slice(v0, v0 + n)
-            for t in range(PACK):
+            for t in ts:
                 nc.scalar.activation(ex_rows[t][:, cols], h2_sums[c, t], ACT.Exp, scale=0.0625)
-            if c == len(Z_CHUNKS) - 1:
-                nc.scalar.activation(ex_plain[:, :, cols], h2_banks[c][:], ACT.Exp, scale=0.0625)
-            else:
-                for t in range(PACK):
+                if c == 0:
                     nc.sync.dma_start(ex_plain[:, t, cols], ex_rows[t][:, cols])
 
-        def negate(c):
+        def negate(c, ts):
             v0, n = Z_CHUNKS[c]
-            for t in range(PACK):
-                nc.scalar.activation(neg_h2_rows[t][:, v0 : v0 + n], h2_sums[c, t], ACT.Copy, scale=-0.0625)
+            for t in ts:
+                if c == 1:
+                    nc.vector.tensor_scalar_mul(neg_h2_rows[t][:, v0 : v0 + n], h2_sums[c, t], -0.0625)
+                else:
+                    nc.scalar.activation(neg_h2_rows[t][:, v0 : v0 + n], h2_sums[c, t], ACT.Copy, scale=-0.0625)
 
-        last_unit = {c: u for u, (c, ts) in enumerate(units)}
-        for step in range(len(units) + 4):
-            if step < len(units):
-                line_up(step)
-            if 0 <= step - 1 < len(units):
-                differ(step - 1)
-            if 0 <= step - 2 < len(units):
+        first_product((0, 0), (1, 0), (0, 1), (1, 1), (2, 0), (2, 1))
+        for step in range(len(units) - 1):
+            line_up(step)
+            if step >= 2:
                 combine(step - 2)
-            for c, u in last_unit.items():
-                if step == u + 3:
-                    exponentiate(c)
-                if step == u + 4:
-                    negate(c)
+            if step >= 1:
+                differ(step - 1)
+            if step < PE_UNITS:
+                add_up(step)
+            if step >= 2 and units[step - 2][1][-1] == PACK - 1:
+                second_product(units[step - 2][0])
+            if step == 0:
+                first_product((3, 0), (3, 1))
+            if step == 6:
+                exponentiate(0, (0, 1))
+        line_up(7)
+        differ(6)
+        differ(7)
+        combine(5)
+        add_up(7)
+        combine(6)
+        combine(7)
+        second_product(1)
+        second_product(2)
+        exponentiate(0, (2, 3))
+        negate(0, (0, 1, 2))
+        negate(1, range(PACK))
+        for t in range(PACK):
+            exponentiate(1, (t,))
+            exponentiate(2, (t,))
+        for c in (1, 2):
+            v0, n = Z_CHUNKS[c]
+            nc.scalar.activation(ex_plain[:, :, v0 : v0 + n], h2_banks[c][:], ACT.Exp, scale=0.0625)
+        negate(0, (3,))
+        negate(2, range(PACK))
 
         log_sum = held.tile([P, PACK, V], F32)
         for half in range(V // HALF):
@@ -235,7 +269,7 @@ def tile_picked_codepgaplse_none_po_kernel(tc, x_words, x_scales, d_words, d_sca
                 nc.vector.tensor_tensor(y[:, t, :], neg_h2_rows[t][:].indirect(entries(n3_list, v0, n)), log_sum[:, t, cols], ALU.add)
             nc.sync.dma_start(out_rows[:, :, cols], y[:])
             y_grouped = held.tile([P, n, PACK], BF16, name=f"y_grouped{j}", align_bytes=64)
-            interleave(nc.vector.tensor_copy if j == len(OUT_PIECES) - 1 else nc.scalar.copy, y_grouped, y)
+            interleave(nc.vector.tensor_copy if j == len(OUT_PIECES) - 1 else nc.scalar.copy, y_grouped[:], y[:])
             y_words = held.tile([P, n], U32, name=f"y_words{j}", align_bytes=64)
             nc.vector.quantize_mx(y_words[:].bitcast(FP8X4), y_scales[:, cols], y_grouped[:].rearrange("p v t -> p (v t)"))
             nc.sync.dma_start(out_words[:, cols], y_words[:].bitcast(I32))

@@ -19,10 +19,11 @@ ACT = mybir.ActivationFunctionType
 P = 128
 PACK = 4
 BANK = 512
-Z_CHUNKS = ((0, 256), (256, 128), (384, 128))
-OUT_PIECES = ((0, 256), (256, 128), (384, 128))
-HALF = 256
-PE_UNITS = 7
+QUADRANT = 32
+SIXTEENTH = 0.0625
+HALF = V // 2
+CHUNKS = ((0, 256), (256, 128), (384, 128))
+SLOTS = 3
 
 
 def entries(offsets, first, count):
@@ -33,151 +34,169 @@ def interleave(engine_copy, dst, src):
     engine_copy(dst.rearrange("p (c i) t -> p c t i", i=4), src.rearrange("p t (c i) -> p c t i", i=4))
 
 
-def tile_picked_codepgaplse_none_po_kernel(tc, x_words, x_scales, d_words, d_scales, gs, offs, k1, n1, k2, n2, n3, out_0, out_1, out_2):
+def tile_picked_codepgaplse_none_po_kernel(
+    tc, x_words, x_scales, d_words, d_scales, gs, offs, k1, n1, k2, n2, n3, out_0, out_1, out_2
+):
     nc = tc.nc
     with ExitStack() as ctx:
         held = ctx.enter_context(tc.tile_pool(name="held", bufs=1))
         ring = ctx.enter_context(tc.tile_pool(name="ring", bufs=2))
         psum = ctx.enter_context(tc.psum_pool(name="psum", bufs=8))
 
+        def load_scale_table(name, src, clearing_engine):
+            tile = held.tile([P, src.shape[2]], U8, name=name, tag=name, align_bytes=64)
+            clearing_engine.memset(tile[:].bitcast(I32), 0)
+            nc.sync.dma_start(tile[0:P:8, :].bitcast(I32), src[0].bitcast(I32))
+            return tile
+
         def load_list(name, src):
             tile = held.tile(list(src.shape), U16, name=name)
             nc.sync.dma_start(tile[:], src)
             return tile
 
-        def load_words(name, src):
+        def load_word_table(name, src):
             tile = held.tile([P, src.shape[2]], I32, name=name, tag=name, align_bytes=64)
             nc.sync.dma_start(tile[:], src[0].rearrange("p n t -> p (n t)").bitcast(I32))
             return tile
 
-        d_scale_table = held.tile([P, G], U8, tag="d_scale_table", align_bytes=64)
-        nc.gpsimd.memset(d_scale_table[:].bitcast(I32), 0)
-        nc.sync.dma_start(d_scale_table[0:P:8, :].bitcast(I32), d_scales[0].bitcast(I32))
-        x_scale_table = held.tile([P, T], U8, align_bytes=64)
-        nc.vector.memset(x_scale_table[:].bitcast(I32), 0)
-        nc.sync.dma_start(x_scale_table[0:P:8, :].bitcast(I32), x_scales[0].bitcast(I32))
+        d_scale_table = load_scale_table("d_scale_table", d_scales, nc.gpsimd)
+        x_scale_table = load_scale_table("x_scale_table", x_scales, nc.vector)
         k1_list = load_list("k1_list", k1)
         k2_list = load_list("k2_list", k2)
         offs_list = load_list("offs_list", offs)
         n1_list = load_list("n1_list", n1)
         n2_list = load_list("n2_list", n2)
         n3_list = load_list("n3_list", n3)
-        d_table = load_words("d_table", d_words)
-        x_table = load_words("x_table", x_words)
+        d_word_table = load_word_table("d_word_table", d_words)
+        x_word_table = load_word_table("x_word_table", x_words)
 
-        placed_scales = held.tile([P, 2 * H + S], U8, align_bytes=64)
-        nc.gpsimd.memset(placed_scales[:].bitcast(I32), 0)
-        picked_scales = held.tile([P, 2 * H + S], U8, align_bytes=64)
-        nc.vector.tensor_copy(picked_scales[:, 0:H], d_scale_table[:].indirect(k1_list[:]))
-        nc.vector.tensor_copy(picked_scales[:, H : 2 * H], d_scale_table[:].indirect(k2_list[:]))
-        staged_scales = held.tile([P, 2 * H + S], U8, align_bytes=64)
-        nc.vector.tensor_copy(
-            staged_scales[:, 0 : 2 * H].rearrange("p (l t m) -> p l m t", l=2, t=PACK),
-            picked_scales[:, 0 : 2 * H].rearrange("p (l m t) -> p l m t", l=2, t=PACK),
-        )
-        nc.vector.tensor_copy(picked_scales[:, 2 * H :], x_scale_table[:].indirect(offs_list[:]))
-        nc.vector.tensor_copy(staged_scales[:, 2 * H :].bitcast(I32), picked_scales[:, 2 * H :].bitcast(I32))
-        for r in range(4):
-            nc.sync.dma_start(placed_scales[r:P:32, :].bitcast(I32), staged_scales[8 * r : P : 32, :].bitcast(I32))
+        def place_scales(name, picked):
+            placed = held.tile(list(picked.shape), U8, name=name, align_bytes=64)
+            nc.gpsimd.memset(placed[:].bitcast(I32), 0)
+            for r in range(4):
+                nc.sync.dma_start(placed[r:P:QUADRANT, :].bitcast(I32), picked[8 * r : P : QUADRANT, :].bitcast(I32))
+            return placed
 
-        gs_sb = held.tile([P, PACK], F32, tag="d_scale_table", align_bytes=64)
-        nc.sync.dma_start(gs_sb[:], gs.rearrange("(p t) o -> p (t o)", t=PACK))
+        def deal(dst, src):
+            nc.vector.tensor_copy(
+                dst.rearrange("p (l t m) -> p l m t", t=PACK, m=P), src.rearrange("p (l m t) -> p l m t", t=PACK, m=P)
+            )
+
+        picked_w_scales = held.tile([P, 2 * H], U8, align_bytes=64)
+        dealt_w_scales = held.tile([P, 2 * H], U8, align_bytes=64)
+        nc.vector.tensor_copy(picked_w_scales[:, 0:H], d_scale_table[:].indirect(k1_list[:]))
+        nc.vector.tensor_copy(picked_w_scales[:, H:], d_scale_table[:].indirect(k2_list[:]))
+        deal(dealt_w_scales[:], picked_w_scales[:])
+        gs_rows = held.tile([P, PACK], F32, tag="d_scale_table", align_bytes=64)
+        nc.sync.dma_start(gs_rows[:], gs.rearrange("(p t) o -> p (t o)", t=PACK))
+        w_scales = place_scales("w_scales", dealt_w_scales)
+        picked_x_scales = held.tile([P, S], U8, align_bytes=64)
+        nc.vector.tensor_copy(picked_x_scales[:], x_scale_table[:].indirect(offs_list[:]))
+        xq_scales = place_scales("xq_scales", picked_x_scales)
+
         row_factor = held.tile([P, PACK], F32)
         row_sign = held.tile([P, PACK], F32)
-        nc.scalar.activation(row_factor[:], gs_sb[:], ACT.Copy, scale=0.0625 * 0.25)
-        nc.scalar.activation(row_sign[:], gs_sb[:], ACT.Sign)
+        nc.scalar.activation(row_factor[:], gs_rows[:], ACT.Copy, scale=SIXTEENTH * 0.25)
+        nc.scalar.activation(row_sign[:], gs_rows[:], ACT.Sign)
 
         identity = held.tile([P, P], F32)
         make_identity(nc, identity[:])
 
-        def pick_weights(name, k_list, slot):
-            picked = held.tile([P, H], U32, name=name + "_picked", tag=slot, align_bytes=64)
+        def pick_weight_words(name, k_list, tag):
+            picked = held.tile([P, H], U32, name=name + "_picked", tag=tag, align_bytes=64)
             dealt = held.tile([P, H], U32, name=name + "_dealt", align_bytes=64)
-            nc.vector.tensor_copy(picked[:], d_table[:].bitcast(U32).indirect(k_list[:]))
-            nc.vector.tensor_copy(dealt[:].rearrange("p (t m) -> p m t", t=PACK), picked[:].rearrange("p (m t) -> p m t", t=PACK))
+            nc.vector.tensor_copy(picked[:], d_word_table[:].bitcast(U32).indirect(k_list[:]))
+            deal(dealt[:], picked[:])
             return dealt
 
-        w1_words = pick_weights("w1", k1_list, "w1_picked")
+        w1_words = pick_weight_words("w1", k1_list, "w1_picked")
         xq_words = []
-        for half in range(S // BANK):
-            words = held.tile([P, BANK], U32, name=f"xq_words{half}", align_bytes=64)
-            nc.vector.tensor_copy(words[:], x_table[:].bitcast(U32).indirect(entries(offs_list, half * BANK, BANK)))
+        for part in range(S // BANK):
+            words = held.tile([P, BANK], U32, name=f"xq_words{part}", align_bytes=64)
+            nc.vector.tensor_copy(words[:], x_word_table[:].bitcast(U32).indirect(entries(offs_list, part * BANK, BANK)))
             xq_words.append(words)
-        w2_words = pick_weights("w2", k2_list, "x_table")
+        w2_words = pick_weight_words("w2", k2_list, "x_word_table")
 
         h_rows = [held.tile([P, S], F32, name=f"h_rows{t}") for t in range(PACK)]
 
-        def first_product(*parts):
-            for t, half in parts:
+        def first_product(t):
+            for part in range(S // BANK):
+                cols = slice(part * BANK, (part + 1) * BANK)
                 acc = psum.tile([P, BANK], F32, tag="bank")
                 nc.tensor.matmul_mx(
                     acc[:],
                     lhsT=w1_words[:, t * P : (t + 1) * P].bitcast(FP8X4),
-                    lhsT_scale=placed_scales[:, t * P : (t + 1) * P],
-                    rhs=xq_words[half][:].bitcast(FP8X4),
-                    rhs_scale=placed_scales[:, 2 * H + half * BANK : 2 * H + (half + 1) * BANK],
+                    lhsT_scale=w_scales[:, t * P : (t + 1) * P],
+                    rhs=xq_words[part][:].bitcast(FP8X4),
+                    rhs_scale=xq_scales[:, cols],
                     start=True,
                     stop=True,
                 )
-                nc.scalar.activation(h_rows[t][:, half * BANK : (half + 1) * BANK], acc[:], ACT.Copy, scale=row_factor[:, t : t + 1])
+                nc.scalar.activation(h_rows[t][:, cols], acc[:], ACT.Copy, scale=row_factor[:, t : t + 1])
 
+        units = [
+            (c, range(t0, t0 + HALF // n)) for c, (v0, n) in enumerate(CHUNKS) for t0 in range(0, PACK, HALF // n)
+        ]
+        last = len(units) - 1
+        wide, middle, final = range(len(CHUNKS))
         ex_rows = [held.tile([P, V], F32, name=f"ex_rows{t}") for t in range(PACK)]
         neg_h2_rows = [held.tile([P, V], F32, name=f"neg_h2_rows{t}") for t in range(PACK)]
         ex_plain = held.tile([P, PACK, V], F32)
-
-        units = []
-        for c, (v0, n) in enumerate(Z_CHUNKS):
-            per = HALF // n
-            for t0 in range(0, PACK, per):
-                units.append((c, list(range(t0, t0 + per))))
-        z_planes = [held.tile([P, PACK, n], BF16, name=f"z_planes{c}") for c, (v0, n) in enumerate(Z_CHUNKS)]
+        z_planes = [held.tile([P, PACK, n], BF16, name=f"z_planes{c}") for c, (v0, n) in enumerate(CHUNKS)]
         lined, sums, gaps, h2_banks, h2_sums = {}, {}, {}, {}, {}
 
         def line_up(u):
-            c, ts = units[u]
-            v0, n = Z_CHUNKS[c]
-            ln = held.tile([P, 2 * HALF], F32, tag=f"slot{u % 3}" if u < 7 else "z_grouped0", align_bytes=64)
-            for i, t in enumerate(ts):
-                nc.vector.tensor_copy(ln[:, 2 * n * i : 2 * n * (i + 1)], h_rows[t][:].indirect(entries(n1_list, 2 * v0, 2 * n)))
+            c, planes = units[u]
+            v0, n = CHUNKS[c]
+            ln = held.tile([P, 2 * HALF], F32, tag=f"slot{u % SLOTS}" if u < last else f"z_grouped{wide}", align_bytes=64)
+            for i, t in enumerate(planes):
+                nc.vector.tensor_copy(
+                    ln[:, 2 * n * i : 2 * n * (i + 1)], h_rows[t][:].indirect(entries(n1_list, 2 * v0, 2 * n))
+                )
             lined[u] = ln
+
+        def differ(u):
+            diff = held.tile([P, HALF], F32, tag="diff" if u < last else "last_diff")
+            nc.vector.tensor_tensor(diff[:], lined[u][:, 0 : 2 * HALF : 2], lined[u][:, 1 : 2 * HALF : 2], ALU.subtract)
+            gap = held.tile([P, HALF], F32, tag=f"slot{u % SLOTS}" if u + SLOTS < last else f"gap{u}", align_bytes=64)
+            nc.scalar.activation(gap[:], diff[:], ACT.Abs, scale=3.0)
+            gaps[u] = gap
 
         def add_up(u):
             ln = lined[u]
-            if u < PE_UNITS:
-                turned = psum.tile([P, 2, P], F32, tag="bank")
-                for b in range(2):
+            if u < last:
+                turned = psum.tile([P, HALF // P, P], F32, tag="bank")
+                for block in range(HALF // P):
                     for e in range(2):
-                        nc.tensor.matmul(turned[:, b, :], ln[:, 2 * P * b + e : 2 * P * (b + 1) : 2], identity[:], start=e == 0, stop=e == 1, is_transpose=True)
-                turned_sb = ring.tile([P, 2, P], F32, tag="turned_sb")
+                        neighbour = ln[:, 2 * P * block + e : 2 * P * (block + 1) : 2]
+                        nc.tensor.matmul(
+                            turned[:, block, :], neighbour, identity[:], start=e == 0, stop=e == 1, is_transpose=True
+                        )
+                turned_sb = ring.tile([P, HALF // P, P], F32, tag="turned_sb")
                 nc.scalar.copy(turned_sb[:], turned[:])
                 pair_sum = psum.tile([P, HALF], F32, tag="bank")
-                for b in range(2):
-                    nc.tensor.transpose(pair_sum[:, P * b : P * (b + 1)], turned_sb[:, b, :], identity[:])
+                for block in range(HALF // P):
+                    nc.tensor.transpose(pair_sum[:, P * block : P * (block + 1)], turned_sb[:, block, :], identity[:])
             else:
                 pair_sum = ring.tile([P, HALF], F32, tag="pair_sum")
                 nc.vector.tensor_tensor(pair_sum[:], ln[:, 0 : 2 * HALF : 2], ln[:, 1 : 2 * HALF : 2], ALU.add)
             sums[u] = pair_sum
 
-        def differ(u):
-            first, second = lined[u][:, 0 : 2 * HALF : 2], lined[u][:, 1 : 2 * HALF : 2]
-            diff = held.tile([P, HALF], F32, tag="diff" if u < 7 else "last_diff")
-            nc.vector.tensor_tensor(diff[:], first, second, ALU.subtract)
-            gap = held.tile([P, HALF], F32, tag=f"slot{u % 3}" if u + 3 < 7 else f"gap{u}", align_bytes=64)
-            nc.scalar.activation(gap[:], diff[:], ACT.Abs, scale=3.0)
-            gaps[u] = gap
-
         def combine(u):
-            c, ts = units[u]
-            v0, n = Z_CHUNKS[c]
-            for i, t in enumerate(ts):
+            c, planes = units[u]
+            n = CHUNKS[c][1]
+            for i, t in enumerate(planes):
                 cols = slice(n * i, n * (i + 1))
-                nc.vector.scalar_tensor_tensor(z_planes[c][:, t, :], gaps[u][:, cols], row_sign[:, t : t + 1], sums[u][:, cols], ALU.mult, ALU.add)
+                nc.vector.scalar_tensor_tensor(
+                    z_planes[c][:, t, :], gaps[u][:, cols], row_sign[:, t : t + 1], sums[u][:, cols], ALU.mult, ALU.add
+                )
 
         def second_product(c):
-            v0, n = Z_CHUNKS[c]
+            n = CHUNKS[c][1]
             z_grouped = held.tile([P, n, PACK], BF16, name=f"z_grouped{c}", tag=f"z_grouped{c}", align_bytes=64)
+            engine_copy = nc.vector.tensor_copy if c == final else nc.scalar.copy
             for w0 in range(0, n, P):
-                interleave(nc.vector.tensor_copy if c == len(Z_CHUNKS) - 1 else nc.scalar.copy, z_grouped[:, w0 : w0 + P, :], z_planes[c][:, :, w0 : w0 + P])
+                interleave(engine_copy, z_grouped[:, w0 : w0 + P, :], z_planes[c][:, :, w0 : w0 + P])
             z_words = held.tile([P, n], U32, name=f"z_words{c}", align_bytes=64)
             z_scales = held.tile([P, n], U8, name=f"z_scales{c}", align_bytes=64)
             nc.vector.quantize_mx(z_words[:].bitcast(FP8X4), z_scales[:], z_grouped[:].rearrange("p v t -> p (v t)"))
@@ -188,7 +207,7 @@ def tile_picked_codepgaplse_none_po_kernel(tc, x_words, x_scales, d_words, d_sca
                 nc.tensor.matmul_mx(
                     acc[:, t % per_bank, :],
                     lhsT=w2_words[:, t * P : (t + 1) * P].bitcast(FP8X4),
-                    lhsT_scale=placed_scales[:, H + t * P : H + (t + 1) * P],
+                    lhsT_scale=w_scales[:, H + t * P : H + (t + 1) * P],
                     rhs=z_words[:].bitcast(FP8X4),
                     rhs_scale=z_scales[:],
                     start=True,
@@ -197,82 +216,83 @@ def tile_picked_codepgaplse_none_po_kernel(tc, x_words, x_scales, d_words, d_sca
                 h2_sums[c, t] = acc[:, t % per_bank, :]
             h2_banks[c] = acc
 
-        def exponentiate(c, ts):
-            v0, n = Z_CHUNKS[c]
+        def exponentiate(c, planes):
+            v0, n = CHUNKS[c]
             cols = slice(v0, v0 + n)
-            for t in ts:
-                nc.scalar.activation(ex_rows[t][:, cols], h2_sums[c, t], ACT.Exp, scale=0.0625)
-                if c == 0:
+            for t in planes:
+                nc.scalar.activation(ex_rows[t][:, cols], h2_sums[c, t], ACT.Exp, scale=SIXTEENTH)
+                if c == wide:
                     nc.sync.dma_start(ex_plain[:, t, cols], ex_rows[t][:, cols])
 
-        def negate(c, ts):
-            v0, n = Z_CHUNKS[c]
-            for t in ts:
-                if c == 1:
-                    nc.vector.tensor_scalar_mul(neg_h2_rows[t][:, v0 : v0 + n], h2_sums[c, t], -0.0625)
+        def negate(c, planes):
+            v0, n = CHUNKS[c]
+            for t in planes:
+                if c == middle:
+                    nc.vector.tensor_scalar_mul(neg_h2_rows[t][:, v0 : v0 + n], h2_sums[c, t], -SIXTEENTH)
                 else:
-                    nc.scalar.activation(neg_h2_rows[t][:, v0 : v0 + n], h2_sums[c, t], ACT.Copy, scale=-0.0625)
+                    nc.scalar.activation(neg_h2_rows[t][:, v0 : v0 + n], h2_sums[c, t], ACT.Copy, scale=-SIXTEENTH)
 
-        first_product((0, 0), (1, 0), (0, 1), (1, 1), (2, 0), (2, 1))
-        for step in range(len(units) - 1):
-            line_up(step)
-            if step >= 2:
-                combine(step - 2)
-            if step >= 1:
-                differ(step - 1)
-            if step < PE_UNITS:
-                add_up(step)
-            if step >= 2 and units[step - 2][1][-1] == PACK - 1:
-                second_product(units[step - 2][0])
-            if step == 0:
-                first_product((3, 0), (3, 1))
-            if step == 6:
-                exponentiate(0, (0, 1))
-        line_up(7)
-        differ(6)
-        differ(7)
-        combine(5)
-        add_up(7)
-        combine(6)
-        combine(7)
-        second_product(1)
-        second_product(2)
-        exponentiate(0, (2, 3))
-        negate(0, (0, 1, 2))
-        negate(1, range(PACK))
+        for t in range(PACK - 1):
+            first_product(t)
+        for u in range(last):
+            line_up(u)
+            if u >= 2:
+                combine(u - 2)
+            if u >= 1:
+                differ(u - 1)
+            add_up(u)
+            if u == 0:
+                first_product(PACK - 1)
+            if u - 2 == PACK - 1:
+                second_product(wide)
+        exponentiate(wide, (0, 1))
+        line_up(last)
+        differ(last - 1)
+        differ(last)
+        combine(last - 2)
+        add_up(last)
+        combine(last - 1)
+        combine(last)
+        second_product(middle)
+        second_product(final)
+        exponentiate(wide, (2, 3))
+        negate(wide, (0, 1, 2))
+        negate(middle, range(PACK))
         for t in range(PACK):
-            exponentiate(1, (t,))
-            exponentiate(2, (t,))
-        for c in (1, 2):
-            v0, n = Z_CHUNKS[c]
-            nc.scalar.activation(ex_plain[:, :, v0 : v0 + n], h2_banks[c][:], ACT.Exp, scale=0.0625)
-        negate(0, (3,))
-        negate(2, range(PACK))
+            exponentiate(middle, (t,))
+            exponentiate(final, (t,))
+        for c in (middle, final):
+            v0, n = CHUNKS[c]
+            nc.scalar.activation(ex_plain[:, :, v0 : v0 + n], h2_banks[c][:], ACT.Exp, scale=SIXTEENTH)
+        negate(wide, (3,))
+        negate(final, range(PACK))
 
         log_sum = held.tile([P, PACK, V], F32)
-        for half in range(V // HALF):
-            cols = slice(half * HALF, (half + 1) * HALF)
+        for v0 in range(0, V, HALF):
+            cols = slice(v0, v0 + HALF)
             for t0 in range(0, PACK, 2):
-                ex_sum = held.tile([P, 2, HALF], F32, name=f"ex_sum{half}_{t0}")
+                ex_sum = held.tile([P, 2, HALF], F32, name=f"ex_sum{v0}_{t0}")
                 for i in range(2):
-                    t = t0 + i
-                    nc.vector.tensor_tensor(ex_sum[:, i, :], ex_rows[t][:].indirect(entries(n2_list, half * HALF, HALF)), ex_plain[:, t, cols], ALU.add)
+                    looked_up = ex_rows[t0 + i][:].indirect(entries(n2_list, v0, HALF))
+                    nc.vector.tensor_tensor(ex_sum[:, i, :], looked_up, ex_plain[:, t0 + i, cols], ALU.add)
                 nc.scalar.activation(log_sum[:, t0 : t0 + 2, cols], ex_sum[:], ACT.Ln)
 
         out_rows = out_0.rearrange("(p t) v -> p t v", t=PACK)
         out_words = out_1[0].rearrange("p n t -> p (n t)").bitcast(I32)
         y_scales = held.tile([P, V], U8, align_bytes=64)
-        for j, (v0, n) in enumerate(OUT_PIECES):
+        for c, (v0, n) in enumerate(CHUNKS):
             cols = slice(v0, v0 + n)
-            y = held.tile([P, PACK, n], F32, name=f"y{j}")
+            y = held.tile([P, PACK, n], F32, name=f"y{c}")
             for t in range(PACK):
-                nc.vector.tensor_tensor(y[:, t, :], neg_h2_rows[t][:].indirect(entries(n3_list, v0, n)), log_sum[:, t, cols], ALU.add)
+                looked_up = neg_h2_rows[t][:].indirect(entries(n3_list, v0, n))
+                nc.vector.tensor_tensor(y[:, t, :], looked_up, log_sum[:, t, cols], ALU.add)
             nc.sync.dma_start(out_rows[:, :, cols], y[:])
-            y_grouped = held.tile([P, n, PACK], BF16, name=f"y_grouped{j}", align_bytes=64)
-            interleave(nc.vector.tensor_copy if j == len(OUT_PIECES) - 1 else nc.scalar.copy, y_grouped[:], y[:])
-            y_words = held.tile([P, n], U32, name=f"y_words{j}", align_bytes=64)
+            y_grouped = held.tile([P, n, PACK], BF16, name=f"y_grouped{c}", align_bytes=64)
+            interleave(nc.vector.tensor_copy if c == final else nc.scalar.copy, y_grouped[:], y[:])
+            y_words = held.tile([P, n], U32, name=f"y_words{c}", align_bytes=64)
             nc.vector.quantize_mx(y_words[:].bitcast(FP8X4), y_scales[:, cols], y_grouped[:].rearrange("p v t -> p (v t)"))
             nc.sync.dma_start(out_words[:, cols], y_words[:].bitcast(I32))
-        for q in range(4):
+        for q in range(P // QUADRANT):
             queue = nc.scalar if q % 2 else nc.sync
-            queue.dma_start(out_2[0, 4 * q : 4 * q + 4, :].bitcast(I32), y_scales[32 * q : 32 * q + 4, :].bitcast(I32))
+            rows = y_scales[QUADRANT * q : QUADRANT * q + 4, :]
+            queue.dma_start(out_2[0, 4 * q : 4 * q + 4, :].bitcast(I32), rows.bitcast(I32))

from contextlib import ExitStack

import concourse.mybir as mybir
from concourse.masks import make_identity

K, T, S, V, G, H = 512, 2048, 1024, 512, 2048, 512
FLOPS = 2 * K * H * S + 2 * K * H * V

F32 = mybir.dt.float32
BF16 = mybir.dt.bfloat16
I32 = mybir.dt.int32
U32 = mybir.dt.uint32
U16 = mybir.dt.uint16
U8 = mybir.dt.uint8
FP8X4 = mybir.dt.float8_e4m3fn_x4
ALU = mybir.AluOpType
ACT = mybir.ActivationFunctionType

P = 128
PACK = 4
BANK = 512
QUADRANT = 32
SIXTEENTH = 0.0625
HALF = V // 2
CHUNKS = ((0, 256), (256, 128), (384, 128))
SLOTS = 3


def entries(offsets, first, count):
    return offsets[:, first // 16 : (first + count) // 16]


def interleave(engine_copy, dst, src):
    engine_copy(dst.rearrange("p (c i) t -> p c t i", i=4), src.rearrange("p t (c i) -> p c t i", i=4))


def tile_picked_codepgaplse_none_po_kernel(
    tc, x_words, x_scales, d_words, d_scales, gs, offs, k1, n1, k2, n2, n3, out_0, out_1, out_2
):
    nc = tc.nc
    with ExitStack() as ctx:
        held = ctx.enter_context(tc.tile_pool(name="held", bufs=1))
        ring = ctx.enter_context(tc.tile_pool(name="ring", bufs=2))
        psum = ctx.enter_context(tc.psum_pool(name="psum", bufs=8))

        def load_scale_table(name, src, clearing_engine):
            tile = held.tile([P, src.shape[2]], U8, name=name, tag=name, align_bytes=64)
            clearing_engine.memset(tile[:].bitcast(I32), 0)
            nc.sync.dma_start(tile[0:P:8, :].bitcast(I32), src[0].bitcast(I32))
            return tile

        def load_list(name, src):
            tile = held.tile(list(src.shape), U16, name=name)
            nc.sync.dma_start(tile[:], src)
            return tile

        def load_word_table(name, src):
            tile = held.tile([P, src.shape[2]], I32, name=name, tag=name, align_bytes=64)
            nc.sync.dma_start(tile[:], src[0].rearrange("p n t -> p (n t)").bitcast(I32))
            return tile

        d_scale_table = load_scale_table("d_scale_table", d_scales, nc.gpsimd)
        x_scale_table = load_scale_table("x_scale_table", x_scales, nc.vector)
        k1_list = load_list("k1_list", k1)
        k2_list = load_list("k2_list", k2)
        offs_list = load_list("offs_list", offs)
        n1_list = load_list("n1_list", n1)
        n2_list = load_list("n2_list", n2)
        n3_list = load_list("n3_list", n3)
        d_word_table = load_word_table("d_word_table", d_words)
        x_word_table = load_word_table("x_word_table", x_words)

        def place_scales(name, picked):
            placed = held.tile(list(picked.shape), U8, name=name, align_bytes=64)
            nc.gpsimd.memset(placed[:].bitcast(I32), 0)
            for r in range(4):
                nc.sync.dma_start(placed[r:P:QUADRANT, :].bitcast(I32), picked[8 * r : P : QUADRANT, :].bitcast(I32))
            return placed

        def deal(dst, src):
            nc.vector.tensor_copy(
                dst.rearrange("p (l t m) -> p l m t", t=PACK, m=P), src.rearrange("p (l m t) -> p l m t", t=PACK, m=P)
            )

        picked_w_scales = held.tile([P, 2 * H], U8, align_bytes=64)
        dealt_w_scales = held.tile([P, 2 * H], U8, align_bytes=64)
        nc.vector.tensor_copy(picked_w_scales[:, 0:H], d_scale_table[:].indirect(k1_list[:]))
        nc.vector.tensor_copy(picked_w_scales[:, H:], d_scale_table[:].indirect(k2_list[:]))
        deal(dealt_w_scales[:], picked_w_scales[:])
        gs_rows = held.tile([P, PACK], F32, tag="d_scale_table", align_bytes=64)
        nc.sync.dma_start(gs_rows[:], gs.rearrange("(p t) o -> p (t o)", t=PACK))
        w_scales = place_scales("w_scales", dealt_w_scales)
        picked_x_scales = held.tile([P, S], U8, align_bytes=64)
        nc.vector.tensor_copy(picked_x_scales[:], x_scale_table[:].indirect(offs_list[:]))
        xq_scales = place_scales("xq_scales", picked_x_scales)

        row_factor = held.tile([P, PACK], F32)
        row_sign = held.tile([P, PACK], F32)
        nc.scalar.activation(row_factor[:], gs_rows[:], ACT.Copy, scale=SIXTEENTH * 0.25)
        nc.scalar.activation(row_sign[:], gs_rows[:], ACT.Sign)

        identity = held.tile([P, P], F32)
        make_identity(nc, identity[:])

        def pick_weight_words(name, k_list, tag):
            picked = held.tile([P, H], U32, name=name + "_picked", tag=tag, align_bytes=64)
            dealt = held.tile([P, H], U32, name=name + "_dealt", align_bytes=64)
            nc.vector.tensor_copy(picked[:], d_word_table[:].bitcast(U32).indirect(k_list[:]))
            deal(dealt[:], picked[:])
            return dealt

        w1_words = pick_weight_words("w1", k1_list, "w1_picked")
        xq_words = []
        for part in range(S // BANK):
            words = held.tile([P, BANK], U32, name=f"xq_words{part}", align_bytes=64)
            nc.vector.tensor_copy(words[:], x_word_table[:].bitcast(U32).indirect(entries(offs_list, part * BANK, BANK)))
            xq_words.append(words)
        w2_words = pick_weight_words("w2", k2_list, "x_word_table")

        h_rows = [held.tile([P, S], F32, name=f"h_rows{t}") for t in range(PACK)]

        def first_product(t):
            for part in range(S // BANK):
                cols = slice(part * BANK, (part + 1) * BANK)
                acc = psum.tile([P, BANK], F32, tag="bank")
                nc.tensor.matmul_mx(
                    acc[:],
                    lhsT=w1_words[:, t * P : (t + 1) * P].bitcast(FP8X4),
                    lhsT_scale=w_scales[:, t * P : (t + 1) * P],
                    rhs=xq_words[part][:].bitcast(FP8X4),
                    rhs_scale=xq_scales[:, cols],
                    start=True,
                    stop=True,
                )
                nc.scalar.activation(h_rows[t][:, cols], acc[:], ACT.Copy, scale=row_factor[:, t : t + 1])

        units = [
            (c, range(t0, t0 + HALF // n)) for c, (v0, n) in enumerate(CHUNKS) for t0 in range(0, PACK, HALF // n)
        ]
        last = len(units) - 1
        wide, middle, final = range(len(CHUNKS))
        ex_rows = [held.tile([P, V], F32, name=f"ex_rows{t}") for t in range(PACK)]
        neg_h2_rows = [held.tile([P, V], F32, name=f"neg_h2_rows{t}") for t in range(PACK)]
        ex_plain = held.tile([P, PACK, V], F32)
        z_planes = [held.tile([P, PACK, n], BF16, name=f"z_planes{c}") for c, (v0, n) in enumerate(CHUNKS)]
        lined, sums, gaps, h2_banks, h2_sums = {}, {}, {}, {}, {}

        def line_up(u):
            c, planes = units[u]
            v0, n = CHUNKS[c]
            ln = held.tile([P, 2 * HALF], F32, tag=f"slot{u % SLOTS}" if u < last else f"z_grouped{wide}", align_bytes=64)
            for i, t in enumerate(planes):
                nc.vector.tensor_copy(
                    ln[:, 2 * n * i : 2 * n * (i + 1)], h_rows[t][:].indirect(entries(n1_list, 2 * v0, 2 * n))
                )
            lined[u] = ln

        def differ(u):
            diff = held.tile([P, HALF], F32, tag="diff" if u < last else "last_diff")
            nc.vector.tensor_tensor(diff[:], lined[u][:, 0 : 2 * HALF : 2], lined[u][:, 1 : 2 * HALF : 2], ALU.subtract)
            gap = held.tile([P, HALF], F32, tag=f"slot{u % SLOTS}" if u + SLOTS < last else f"gap{u}", align_bytes=64)
            nc.scalar.activation(gap[:], diff[:], ACT.Abs, scale=3.0)
            gaps[u] = gap

        def add_up(u):
            ln = lined[u]
            if u < last:
                turned = psum.tile([P, HALF // P, P], F32, tag="bank")
                for block in range(HALF // P):
                    for e in range(2):
                        neighbour = ln[:, 2 * P * block + e : 2 * P * (block + 1) : 2]
                        nc.tensor.matmul(
                            turned[:, block, :], neighbour, identity[:], start=e == 0, stop=e == 1, is_transpose=True
                        )
                turned_sb = ring.tile([P, HALF // P, P], F32, tag="turned_sb")
                nc.scalar.copy(turned_sb[:], turned[:])
                pair_sum = psum.tile([P, HALF], F32, tag="bank")
                for block in range(HALF // P):
                    nc.tensor.transpose(pair_sum[:, P * block : P * (block + 1)], turned_sb[:, block, :], identity[:])
            else:
                pair_sum = ring.tile([P, HALF], F32, tag="pair_sum")
                nc.vector.tensor_tensor(pair_sum[:], ln[:, 0 : 2 * HALF : 2], ln[:, 1 : 2 * HALF : 2], ALU.add)
            sums[u] = pair_sum

        def combine(u):
            c, planes = units[u]
            n = CHUNKS[c][1]
            for i, t in enumerate(planes):
                cols = slice(n * i, n * (i + 1))
                nc.vector.scalar_tensor_tensor(
                    z_planes[c][:, t, :], gaps[u][:, cols], row_sign[:, t : t + 1], sums[u][:, cols], ALU.mult, ALU.add
                )

        def second_product(c):
            n = CHUNKS[c][1]
            z_grouped = held.tile([P, n, PACK], BF16, name=f"z_grouped{c}", tag=f"z_grouped{c}", align_bytes=64)
            engine_copy = nc.vector.tensor_copy if c == final else nc.scalar.copy
            for w0 in range(0, n, P):
                interleave(engine_copy, z_grouped[:, w0 : w0 + P, :], z_planes[c][:, :, w0 : w0 + P])
            z_words = held.tile([P, n], U32, name=f"z_words{c}", align_bytes=64)
            z_scales = held.tile([P, n], U8, name=f"z_scales{c}", align_bytes=64)
            nc.vector.quantize_mx(z_words[:].bitcast(FP8X4), z_scales[:], z_grouped[:].rearrange("p v t -> p (v t)"))
            per_bank = BANK // n
            for t in range(PACK):
                if t % per_bank == 0:
                    acc = psum.tile([P, per_bank, n], F32, tag="bank")
                nc.tensor.matmul_mx(
                    acc[:, t % per_bank, :],
                    lhsT=w2_words[:, t * P : (t + 1) * P].bitcast(FP8X4),
                    lhsT_scale=w_scales[:, H + t * P : H + (t + 1) * P],
                    rhs=z_words[:].bitcast(FP8X4),
                    rhs_scale=z_scales[:],
                    start=True,
                    stop=True,
                )
                h2_sums[c, t] = acc[:, t % per_bank, :]
            h2_banks[c] = acc

        def exponentiate(c, planes):
            v0, n = CHUNKS[c]
            cols = slice(v0, v0 + n)
            for t in planes:
                nc.scalar.activation(ex_rows[t][:, cols], h2_sums[c, t], ACT.Exp, scale=SIXTEENTH)
                if c == wide:
                    nc.sync.dma_start(ex_plain[:, t, cols], ex_rows[t][:, cols])

        def negate(c, planes):
            v0, n = CHUNKS[c]
            for t in planes:
                if c == middle:
                    nc.vector.tensor_scalar_mul(neg_h2_rows[t][:, v0 : v0 + n], h2_sums[c, t], -SIXTEENTH)
                else:
                    nc.scalar.activation(neg_h2_rows[t][:, v0 : v0 + n], h2_sums[c, t], ACT.Copy, scale=-SIXTEENTH)

        for t in range(PACK - 1):
            first_product(t)
        for u in range(last):
            line_up(u)
            if u >= 2:
                combine(u - 2)
            if u >= 1:
                differ(u - 1)
            add_up(u)
            if u == 0:
                first_product(PACK - 1)
            if u - 2 == PACK - 1:
                second_product(wide)
        exponentiate(wide, (0, 1))
        line_up(last)
        differ(last - 1)
        differ(last)
        combine(last - 2)
        add_up(last)
        combine(last - 1)
        combine(last)
        second_product(middle)
        second_product(final)
        exponentiate(wide, (2, 3))
        negate(wide, (0, 1, 2))
        negate(middle, range(PACK))
        for t in range(PACK):
            exponentiate(middle, (t,))
            exponentiate(final, (t,))
        for c in (middle, final):
            v0, n = CHUNKS[c]
            nc.scalar.activation(ex_plain[:, :, v0 : v0 + n], h2_banks[c][:], ACT.Exp, scale=SIXTEENTH)
        negate(wide, (3,))
        negate(final, range(PACK))

        log_sum = held.tile([P, PACK, V], F32)
        for v0 in range(0, V, HALF):
            cols = slice(v0, v0 + HALF)
            for t0 in range(0, PACK, 2):
                ex_sum = held.tile([P, 2, HALF], F32, name=f"ex_sum{v0}_{t0}")
                for i in range(2):
                    looked_up = ex_rows[t0 + i][:].indirect(entries(n2_list, v0, HALF))
                    nc.vector.tensor_tensor(ex_sum[:, i, :], looked_up, ex_plain[:, t0 + i, cols], ALU.add)
                nc.scalar.activation(log_sum[:, t0 : t0 + 2, cols], ex_sum[:], ACT.Ln)

        out_rows = out_0.rearrange("(p t) v -> p t v", t=PACK)
        out_words = out_1[0].rearrange("p n t -> p (n t)").bitcast(I32)
        y_scales = held.tile([P, V], U8, align_bytes=64)
        for c, (v0, n) in enumerate(CHUNKS):
            cols = slice(v0, v0 + n)
            y = held.tile([P, PACK, n], F32, name=f"y{c}")
            for t in range(PACK):
                looked_up = neg_h2_rows[t][:].indirect(entries(n3_list, v0, n))
                nc.vector.tensor_tensor(y[:, t, :], looked_up, log_sum[:, t, cols], ALU.add)
            nc.sync.dma_start(out_rows[:, :, cols], y[:])
            y_grouped = held.tile([P, n, PACK], BF16, name=f"y_grouped{c}", align_bytes=64)
            interleave(nc.vector.tensor_copy if c == final else nc.scalar.copy, y_grouped[:], y[:])
            y_words = held.tile([P, n], U32, name=f"y_words{c}", align_bytes=64)
            nc.vector.quantize_mx(y_words[:].bitcast(FP8X4), y_scales[:, cols], y_grouped[:].rearrange("p v t -> p (v t)"))
            nc.sync.dma_start(out_words[:, cols], y_words[:].bitcast(I32))
        for q in range(P // QUADRANT):
            queue = nc.scalar if q % 2 else nc.sync
            rows = y_scales[QUADRANT * q : QUADRANT * q + 4, :]
            queue.dma_start(out_2[0, 4 * q : 4 * q + 4, :].bitcast(I32), rows.bitcast(I32))
